import numpy as np
import ml_dtypes


def mxq(x, axis, fmt="e4m3"):
    dtype, down = {"e4m3": (ml_dtypes.float8_e4m3fn, 7), "e5m2": (ml_dtypes.float8_e5m2, 14)}[fmt]
    v = np.moveaxis(np.asarray(x, np.float32).astype(ml_dtypes.bfloat16).astype(np.float64), axis, -1)
    blocks = v.reshape(v.shape[:-1] + (-1, 32))
    amax = np.abs(blocks).max(-1, keepdims=True)
    byte = np.maximum(np.where(amax > 0, np.frexp(amax)[1] - 1 + 127, 0) - down, 1)
    scale = np.exp2(byte - 127.0)
    codes = (blocks / scale).astype(np.float32).astype(dtype).astype(np.float64)
    return np.moveaxis((codes * scale).reshape(v.shape), -1, axis)


WIDE = False


def mx_kscale(k):
    if not WIDE:
        return np.ones(k)
    levels = np.array([10, -10, 5, -5, 0])
    if k % 512:
        return np.exp2(np.random.permutation(np.resize(levels, k // 32))).repeat(32)
    a = np.empty((k // 512, 16))
    for p in range(k // 512):
        a[p, :8] = np.random.permutation(np.resize(levels, 8))
        for g in range(8):
            far = levels[np.abs(levels - a[p, g]) >= 10]
            a[p, g + 8] = far[np.random.randint(len(far))]
    return np.exp2(a.ravel()).repeat(32)


def f64(x):
    return np.asarray(x).astype(np.float64)


def striped(idx):
    return np.tile(idx.reshape(-1, 16).T, (8, 1)).astype(np.uint16)


def unstriped(offs):
    return offs[:16].T.reshape(-1).astype(np.int64)


def striped8(idx):
    return np.concatenate([x.reshape(-1, 16).T for x in idx]).astype(np.uint16)


def runs(offs, k):
    lists = np.stack([offs[16 * r : 16 * r + 16].T.reshape(-1) for r in range(8)]).astype(np.int64)
    return lists[np.arange(k) % 512 // 64]


def pack_weight(w):
    k, n = w.shape
    w = f64(np.asarray(w, np.float32).astype(ml_dtypes.bfloat16)).reshape(k // 32, 32, n)
    amax = np.abs(w).max(1)
    byte = np.clip(np.where(amax > 0, np.frexp(amax)[1] - 1 + 127 - 7, 1), 1, 254)
    scaled = (w * np.exp2(127.0 - byte)[:, None, :]).reshape(k, n).astype(np.float32)
    words = np.ascontiguousarray(scaled.reshape(k // 512, 128, 4, n).transpose(0, 1, 3, 2)).astype(ml_dtypes.float8_e4m3fn).view(np.uint8)
    return words, np.ascontiguousarray(byte.astype(np.uint8).reshape(k // 512, 16, n))


def unpack_weight(words, scales):
    g, p, n, _ = words.shape
    vals = np.ascontiguousarray(words).view(ml_dtypes.float8_e4m3fn).astype(np.float64) * np.repeat(np.exp2(scales.astype(np.float64) - 127.0), 8, axis=1)[..., None]
    return vals.transpose(0, 1, 3, 2).reshape(g * 512, n)


K, T, S, N, G, H = 512, 2048, 512, 512, 2048, 512


def setup_inputs():
    n = np.random.standard_normal
    s = mx_kscale(K)[:, None]
    u = mx_kscale(S)
    packed_xT = pack_weight(n((K, T)) * s)
    packed_dT = pack_weight(n((K, G)) / s)
    return {
        "x_words": packed_xT[0],
        "x_scales": packed_xT[1],
        "d_words": packed_dT[0],
        "d_scales": packed_dT[1],
        "gn": (np.random.uniform(0.5, 1.5, (H, 1)) * u[:, None]).astype(np.float32),
        "w1": (n((H, N)) / np.sqrt(2 * H) / u[:, None]).astype(np.float32),
        "w2": (n((K, N)) / np.sqrt(2 * K) / s).astype(np.float32),
        "offs": striped(np.random.permutation(T)[:S]),
        "k1": striped8(np.random.randint(0, G, (8, H))),
        "n1": striped8(np.stack([np.random.permutation(S) for _ in range(8)])),
        "n2": striped8(np.stack([np.random.permutation(S) for _ in range(8)])),
        "two": striped(np.random.permutation(T)[:S]),
        "n3": striped(np.random.randint(0, S, G)),
    }


def reference(x_words, x_scales, d_words, d_scales, gn, w1, w2, offs, k1, n1, n2, two, n3):
    d_k1 = unpack_weight(d_words, d_scales)[np.arange(K)[:, None], runs(k1, K)]
    xq = unpack_weight(x_words, x_scales)[:, unstriped(offs)]
    s = 0.0625 * (d_k1.T @ xq)
    z = f64(gn) * ((s * (s[np.arange(H)[:, None], runs(n1, H)])) * (np.tanh(s[np.arange(H)[:, None], runs(n2, H)])))
    x_two = unpack_weight(x_words, x_scales)[:, unstriped(two)]
    h = mxq(f64(w1), 0, "e4m3").T @ mxq(z, 0, "e4m3") + mxq(f64(w2), 0, "e4m3").T @ x_two
    mb = h[:, unstriped(n3)]
    mx = mb.reshape(N, S, 4).max(axis=2)
    return h - mx

@@ -1,0 +1,266 @@
+from contextlib import ExitStack
+
+import concourse.mybir as mybir
+
+K, T, S, N, G, H = 512, 2048, 512, 512, 2048, 512
+FLOPS = 3 * 2 * 512 * 512 * 512
+
+F32 = mybir.dt.float32
+BF16 = mybir.dt.bfloat16
+U32 = mybir.dt.uint32
+I32 = mybir.dt.int32
+U16 = mybir.dt.uint16
+U8 = mybir.dt.uint8
+FP8X4 = mybir.dt.float8_e4m3fn_x4
+ALU = mybir.AluOpType
+ACT = mybir.ActivationFunctionType
+
+P = 128
+PACK = 4
+HALF = S // 2
+MEMBERS = 4
+
+
+def entries(list_tile, first, count):
+    return list_tile[:, first // 16 : (first + count) // 16]
+
+
+def tile_picked_kmixcubegmaxd_none_p_kernel(
+    tc, x_words, x_scales, d_words, d_scales, gn, w1, w2, offs, k1, n1, n2, two, n3, out
+):
+    nc = tc.nc
+    with ExitStack() as ctx:
+        keep = ctx.enter_context(tc.tile_pool(name="keep", bufs=1))
+        psum = ctx.enter_context(tc.psum_pool(name="psum", bufs=1))
+
+        def list_tile(name, src):
+            tile = keep.tile(list(src.shape), U16, name=name)
+            nc.sync.dma_start(tile[:], src)
+            return tile
+
+        def words_i32(src):
+            return src[0].rearrange("p n t -> p (n t)").bitcast(I32)
+
+        d_byte_tab = keep.tile([P, G], U8, name="d_byte_tab", align_bytes=64)
+        x_byte_tab = keep.tile([P, T], U8, name="x_byte_tab", align_bytes=64)
+        d_plane = keep.tile([P, H], U8, name="d_plane", align_bytes=64)
+        nc.gpsimd.memset(x_byte_tab[:].bitcast(I32), 0)
+        nc.vector.memset(d_plane[:].bitcast(I32), 0)
+
+        k1_t = list_tile("k1_t", k1)
+        nc.sync.dma_start(
+            d_byte_tab[:].bitcast(I32), d_scales[0].bitcast(I32).unsqueeze(1).to_broadcast([16, 8, G // 4])
+        )
+        d_word_tab = keep.tile([P, G], U32, name="d_word_tab", align_bytes=64)
+        nc.sync.dma_start(d_word_tab[:].bitcast(I32), words_i32(d_words))
+        for q in range(4):
+            (nc.gpsimd if q < 2 else nc.scalar).dma_start(
+                x_byte_tab[:].bitcast(I32)[32 * q : 32 * q + 4, :],
+                x_scales[0].bitcast(I32)[4 * q : 4 * q + 4, :],
+            )
+        offs_t = list_tile("offs_t", offs)
+        two_t = list_tile("two_t", two)
+        n1_t = list_tile("n1_t", n1)
+        n2_t = list_tile("n2_t", n2)
+        n3_t = list_tile("n3_t", n3)
+        x_word_tab = keep.tile([P, T], U32, name="x_word_tab", align_bytes=64)
+        nc.sync.dma_start(x_word_tab[:].bitcast(I32), words_i32(x_words))
+        gain = keep.tile([P, PACK], F32, name="gain")
+        nc.gpsimd.dma_start(gain[:], gn.rearrange("(p t) o -> p (t o)", t=PACK))
+
+        d_bytes = keep.tile([P, H], U8, name="d_bytes", align_bytes=64)
+        nc.vector.tensor_copy(d_bytes[:], d_byte_tab[:].indirect(k1_t[:]))
+        d_bytes_dealt = keep.tile([P, H], U8, name="d_bytes_dealt", tag="early_b", align_bytes=64)
+        nc.vector.tensor_copy(
+            d_bytes_dealt[:].rearrange("p (t m) -> p t m", t=PACK),
+            d_bytes[:].rearrange("p (m t) -> p t m", t=PACK),
+        )
+        for a in range(4):
+            nc.scalar.dma_start(
+                d_plane[:].bitcast(I32)[a:P:32, :],
+                d_bytes_dealt[:].bitcast(I32)[8 * a : P : 32, :],
+            )
+        w_raw = keep.tile([P, 2 * PACK * N], F32, name="w_raw", tag="early_b", align_bytes=64)
+        w2_raw = w_raw[:, : PACK * N].rearrange("p (j n) -> p j n", j=PACK)
+        w1_raw = w_raw[:, PACK * N :].rearrange("p (j n) -> p j n", j=PACK)
+        nc.sync.dma_start(w2_raw, w2.rearrange("(p j) n -> p j n", j=PACK))
+        nc.sync.dma_start(w1_raw, w1.rearrange("(p j) n -> p j n", j=PACK))
+
+        d_picked = keep.tile([P, H], U32, name="d_picked", align_bytes=64)
+        nc.vector.tensor_copy(d_picked[:], d_word_tab[:].indirect(k1_t[:]))
+        d_dealt = keep.tile([P, H], U32, name="d_dealt", align_bytes=64)
+        nc.vector.tensor_copy(
+            d_dealt[:].rearrange("p (t c i) -> p c t i", t=PACK, i=4),
+            d_picked[:].rearrange("p (c i t) -> p c t i", t=PACK, i=4),
+        )
+        xq_plane = keep.tile([P, S], U8, name="xq_plane", align_bytes=64)
+        nc.vector.tensor_copy(xq_plane[:], x_byte_tab[:].indirect(offs_t[:]))
+        xq_words = keep.tile([P, S], U32, name="xq_words", align_bytes=64)
+        nc.vector.tensor_copy(xq_words[:], x_word_tab[:].indirect(offs_t[:]))
+
+        s_bank = [psum.tile([P, S], F32, name="s_bank%d" % t) for t in range(PACK)]
+        for t in range(PACK):
+            cols = slice(P * t, P * (t + 1))
+            nc.tensor.matmul_mx(
+                s_bank[t][:],
+                lhsT=d_dealt[:, cols].bitcast(FP8X4),
+                lhsT_scale=d_plane[:, cols],
+                rhs=xq_words[:].bitcast(FP8X4),
+                rhs_scale=xq_plane[:],
+                start=True,
+                stop=True,
+            )
+
+        x2_words = keep.tile([P, S], U32, name="x2_words", align_bytes=64)
+        nc.vector.tensor_copy(x2_words[:], x_word_tab[:].indirect(two_t[:]))
+        x2_plane = keep.tile([P, S], U8, name="x2_plane", align_bytes=64)
+        nc.vector.tensor_copy(x2_plane[:], x_byte_tab[:].indirect(two_t[:]))
+
+        def interleaved(dst, src):
+            return (
+                dst.rearrange("p (c i) t -> p c t i", i=4),
+                src.rearrange("p t (c i) -> p c t i", i=4),
+            )
+
+        def quantise(codes, plane, grouped):
+            nc.vector.quantize_mx(codes.bitcast(FP8X4), plane, grouped.rearrange("p n t -> p (n t)"))
+
+        w2_grouped = keep.tile([P, N, PACK], BF16, name="w2_grouped", align_bytes=64)
+        nc.vector.tensor_copy(*interleaved(w2_grouped[:], w2_raw))
+
+        s_row = [keep.tile([P, S], F32, name="s_row%d" % t) for t in range(PACK)]
+        tanh_row = [keep.tile([P, S], F32, name="tanh_row%d" % t) for t in range(PACK)]
+        s_at_n1 = [[keep.tile([P, HALF], F32, name="s_at_n1_%d%d" % (t, u)) for u in range(2)] for t in range(PACK)]
+        pair = [[keep.tile([P, HALF], F32, name="pair_%d%d" % (t, u)) for u in range(2)] for t in range(PACK)]
+        z_half = [keep.tile([P, PACK, HALF], F32, name="z_half%d" % u) for u in range(2)]
+        z_grouped = [keep.tile([P, HALF, PACK], BF16, name="z_grouped%d" % u, align_bytes=64) for u in range(2)]
+        z_words = [keep.tile([P, HALF], U32, name="z_words%d" % u, align_bytes=64) for u in range(2)]
+        z_plane = [keep.tile([P, HALF], U8, name="z_plane%d" % u, align_bytes=64) for u in range(2)]
+        w_words = [keep.tile([P, N], U32, name="w_words%d" % i, align_bytes=64) for i in range(2)]
+        w_plane = [keep.tile([P, N], U8, name="w_plane%d" % i, align_bytes=64) for i in range(2)]
+
+        def fetch(t, u):
+            nc.scalar.activation(s_at_n1[t][u][:], s_row[t][:].indirect(entries(n1_t, u * HALF, HALF)), ACT.Copy)
+            nc.vector.tensor_tensor(
+                pair[t][u][:], tanh_row[t][:].indirect(entries(n2_t, u * HALF, HALF)), s_at_n1[t][u][:], ALU.mult
+            )
+
+        def finish(t, u):
+            nc.vector.scalar_tensor_tensor(
+                z_half[u][:, t, :],
+                s_row[t][:, u * HALF : (u + 1) * HALF],
+                gain[:, t : t + 1],
+                pair[t][u][:],
+                ALU.mult,
+                ALU.mult,
+            )
+
+        h_bank = [psum.tile([P, S], F32, name="h_bank%d" % t) for t in range(N // P)]
+
+        for t in range(PACK):
+            nc.scalar.activation(tanh_row[t][:], s_bank[t][:], ACT.Tanh, scale=0.0625)
+            nc.scalar.activation(s_row[t][:], s_bank[t][:], ACT.Copy, scale=0.0625)
+            fetch(t, 0)
+            if t == 0:
+                quantise(w_words[1][:], w_plane[1][:], w2_grouped[:])
+            else:
+                finish(t - 1, 0)
+        for mt in range(N // P):
+            cols = slice(P * mt, P * (mt + 1))
+            nc.tensor.matmul_mx(
+                h_bank[mt][:],
+                lhsT=w_words[1][:, cols].bitcast(FP8X4),
+                lhsT_scale=w_plane[1][:, cols],
+                rhs=x2_words[:].bitcast(FP8X4),
+                rhs_scale=x2_plane[:],
+                start=True,
+                stop=False,
+            )
+        for t in range(PACK):
+            fetch(t, 1)
+            if t == 0:
+                finish(PACK - 1, 0)
+            else:
+                finish(t - 1, 1)
+        w1_grouped = keep.tile([P, N, PACK], BF16, name="w1_grouped", align_bytes=64)
+        nc.scalar.copy(*interleaved(w1_grouped[:], w1_raw))
+        nc.scalar.copy(*interleaved(z_grouped[0][:], z_half[0][:]))
+        quantise(w_words[0][:], w_plane[0][:], w1_grouped[:])
+        finish(PACK - 1, 1)
+        quantise(z_words[0][:], z_plane[0][:], z_grouped[0][:])
+        nc.vector.tensor_copy(*interleaved(z_grouped[1][:], z_half[1][:]))
+        quantise(z_words[1][:], z_plane[1][:], z_grouped[1][:])
+        for u in range(2):
+            for mt in range(N // P):
+                cols = slice(P * mt, P * (mt + 1))
+                nc.tensor.matmul_mx(
+                    h_bank[mt][:, u * HALF : (u + 1) * HALF],
+                    lhsT=w_words[0][:, cols].bitcast(FP8X4),
+                    lhsT_scale=w_plane[0][:, cols],
+                    rhs=z_words[u][:].bitcast(FP8X4),
+                    rhs_scale=z_plane[u][:],
+                    start=False,
+                    stop=(u == 1),
+                )
+
+        h_row = [keep.tile([P, S], F32, name="h_row%d" % t) for t in range(N // P)]
+        members = [keep.tile([P, G], F32, name="members%d" % t) for t in range(N // P)]
+        max2 = [keep.tile([P, G // 2], F32, name="max2_%d" % t) for t in range(N // P)]
+        max4 = [keep.tile([P, S], F32, name="max4_%d" % t) for t in range(N // P)]
+        result = [keep.tile([P, S], F32, name="result%d" % t) for t in range(N // P)]
+
+        def gather(on_vector, mt, first, count):
+            src = h_row[mt][:].indirect(entries(n3_t, first, count))
+            dst = members[mt][:, first : first + count]
+            if on_vector:
+                nc.vector.tensor_copy(dst, src)
+            else:
+                nc.scalar.activation(dst, src, ACT.Copy)
+
+        def step1(mt, j0, j1):
+            g = members[mt][:, 4 * j0 : 4 * j1].rearrange("p (j a b) -> p j a b", a=2, b=2)
+            nc.vector.tensor_tensor(
+                max2[mt][:, 2 * j0 : 2 * j1].rearrange("p (j b) -> p j b", b=2), g[:, :, 0, :], g[:, :, 1, :], ALU.max
+            )
+
+        def step2(mt, j0, j1):
+            g = max2[mt][:, 2 * j0 : 2 * j1].rearrange("p (j b) -> p j b", b=2)
+            nc.vector.tensor_tensor(max4[mt][:, j0:j1], g[:, :, 0], g[:, :, 1], ALU.max)
+
+        def step3(mt, j0, j1):
+            nc.vector.tensor_tensor(result[mt][:, j0:j1], h_row[mt][:, j0:j1], max4[mt][:, j0:j1], ALU.subtract)
+            nc.sync.dma_start(out[P * mt : P * (mt + 1), j0:j1], result[mt][:, j0:j1])
+
+        def gather_span(on_vector, mt, first, end):
+            while first < end:
+                count = min(416, end - first)
+                gather(on_vector, mt, first, count)
+                first = first + count
+
+        nc.vector.tensor_copy(h_row[0][:], h_bank[0][:])
+        nc.scalar.copy(h_row[1][:], h_bank[1][:])
+        nc.vector.tensor_copy(h_row[3][:], h_bank[3][:])
+        gather_span(False, 1, 0, G)
+        gather_span(True, 0, 0, G)
+        nc.scalar.copy(h_row[2][:], h_bank[2][:])
+        gather_span(False, 2, 0, G)
+        step1(0, 0, S)
+        step1(1, 0, S)
+        step2(0, 0, S)
+        step2(1, 0, S)
+        step3(0, 0, S)
+        step3(1, 0, S)
+        gather_span(True, 3, 0, 384)
+        gather_span(False, 3, 384, G)
+        step1(2, 0, S)
+        step1(3, 0, 192)
+        step2(2, 0, S)
+        step2(3, 0, 192)
+        step3(2, 0, S)
+        step1(3, 192, 384)
+        step3(3, 0, 192)
+        step2(3, 192, 384)
+        step1(3, 384, S)
+        step3(3, 192, 384)
+        step2(3, 384, S)
+        step3(3, 384, S)

@@ -17,8 +17,9 @@ ACT = mybir.ActivationFunctionType
 
 P = 128
 PACK = 4
-HALF = S // 2
+PIECES = ((0, 256), (256, 512))
 MEMBERS = 4
+H_WINDOW = 1056
 
 
 def entries(list_tile, first, count):
@@ -38,67 +39,71 @@ def tile_picked_kmixcubegmaxd_none_p_kernel(
             nc.sync.dma_start(tile[:], src)
             return tile
 
-        def words_i32(src):
-            return src[0].rearrange("p n t -> p (n t)").bitcast(I32)
+        def word_table(name, src):
+            tile = keep.tile([P, T], U32, name=name, tag=name, align_bytes=64)
+            nc.sync.dma_start(tile[:].bitcast(I32), src[0].rearrange("p n t -> p (n t)").bitcast(I32))
+            return tile
 
-        d_byte_tab = keep.tile([P, G], U8, name="d_byte_tab", align_bytes=64)
-        x_byte_tab = keep.tile([P, T], U8, name="x_byte_tab", align_bytes=64)
-        d_plane = keep.tile([P, H], U8, name="d_plane", align_bytes=64)
-        nc.gpsimd.memset(x_byte_tab[:].bitcast(I32), 0)
-        nc.vector.memset(d_plane[:].bitcast(I32), 0)
+        def byte_table(name, src):
+            tile = keep.tile([P, T], U8, name=name, tag=name, align_bytes=64)
+            nc.sync.dma_start(tile[:].bitcast(I32), src[0].bitcast(I32).unsqueeze(1).to_broadcast([16, 8, T // 4]))
+            return tile
+
+        planes = keep.tile([P, 2 * S], U8, name="planes", align_bytes=64)
+        nc.vector.memset(planes[:].bitcast(I32), 0)
+        x2_plane = keep.tile([P, S], U8, name="x2_plane", align_bytes=64)
+        nc.vector.memset(x2_plane[:].bitcast(I32), 0)
 
         k1_t = list_tile("k1_t", k1)
-        nc.sync.dma_start(
-            d_byte_tab[:].bitcast(I32), d_scales[0].bitcast(I32).unsqueeze(1).to_broadcast([16, 8, G // 4])
-        )
-        d_word_tab = keep.tile([P, G], U32, name="d_word_tab", align_bytes=64)
-        nc.sync.dma_start(d_word_tab[:].bitcast(I32), words_i32(d_words))
-        for q in range(4):
-            (nc.gpsimd if q < 2 else nc.scalar).dma_start(
-                x_byte_tab[:].bitcast(I32)[32 * q : 32 * q + 4, :],
-                x_scales[0].bitcast(I32)[4 * q : 4 * q + 4, :],
-            )
+        d_byte_tab = byte_table("d_byte_tab", d_scales)
         offs_t = list_tile("offs_t", offs)
+        x_byte_tab = byte_table("x_byte_tab", x_scales)
         two_t = list_tile("two_t", two)
+        d_word_tab = word_table("d_word_tab", d_words)
         n1_t = list_tile("n1_t", n1)
         n2_t = list_tile("n2_t", n2)
+        x_word_tab = word_table("x_word_tab", x_words)
         n3_t = list_tile("n3_t", n3)
-        x_word_tab = keep.tile([P, T], U32, name="x_word_tab", align_bytes=64)
-        nc.sync.dma_start(x_word_tab[:].bitcast(I32), words_i32(x_words))
         gain = keep.tile([P, PACK], F32, name="gain")
-        nc.gpsimd.dma_start(gain[:], gn.rearrange("(p t) o -> p (t o)", t=PACK))
+        nc.sync.dma_start(gain[:], gn.rearrange("(p t) o -> p (t o)", t=PACK))
 
-        d_bytes = keep.tile([P, H], U8, name="d_bytes", align_bytes=64)
-        nc.vector.tensor_copy(d_bytes[:], d_byte_tab[:].indirect(k1_t[:]))
-        d_bytes_dealt = keep.tile([P, H], U8, name="d_bytes_dealt", tag="early_b", align_bytes=64)
-        nc.vector.tensor_copy(
-            d_bytes_dealt[:].rearrange("p (t m) -> p t m", t=PACK),
-            d_bytes[:].rearrange("p (m t) -> p t m", t=PACK),
-        )
-        for a in range(4):
-            nc.scalar.dma_start(
-                d_plane[:].bitcast(I32)[a:P:32, :],
-                d_bytes_dealt[:].bitcast(I32)[8 * a : P : 32, :],
-            )
-        w_raw = keep.tile([P, 2 * PACK * N], F32, name="w_raw", tag="early_b", align_bytes=64)
-        w2_raw = w_raw[:, : PACK * N].rearrange("p (j n) -> p j n", j=PACK)
-        w1_raw = w_raw[:, PACK * N :].rearrange("p (j n) -> p j n", j=PACK)
-        nc.sync.dma_start(w2_raw, w2.rearrange("(p j) n -> p j n", j=PACK))
-        nc.sync.dma_start(w1_raw, w1.rearrange("(p j) n -> p j n", j=PACK))
+        picked_bytes = keep.tile([P, 2 * S], U8, name="picked_bytes", align_bytes=64)
+        x2_bytes = keep.tile([P, S], U8, name="x2_bytes", align_bytes=64)
+        nc.vector.tensor_copy(picked_bytes[:, 0:S], d_byte_tab[:].indirect(k1_t[:]))
+        nc.vector.tensor_copy(picked_bytes[:, S : 2 * S], x_byte_tab[:].indirect(offs_t[:]))
+
+        def move_rows(queue, dst, src):
+            for a in range(4):
+                queue.dma_start(
+                    dst[:].bitcast(I32)[a:P:32, :],
+                    src[:].bitcast(I32)[8 * a : P : 32, :],
+                )
+
+        move_rows(nc.scalar, planes, picked_bytes)
+        nc.vector.tensor_copy(x2_bytes[:], x_byte_tab[:].indirect(two_t[:]))
+        move_rows(nc.sync, x2_plane, x2_bytes)
+        w2_raw = keep.tile([P, PACK, N], F32, name="w2_raw", tag="x_byte_tab", align_bytes=64)
+        nc.sync.dma_start(w2_raw[:], w2.rearrange("(p j) n -> p j n", j=PACK))
+        xq_plane = planes[:, S : 2 * S]
 
         d_picked = keep.tile([P, H], U32, name="d_picked", align_bytes=64)
         nc.vector.tensor_copy(d_picked[:], d_word_tab[:].indirect(k1_t[:]))
+        w1_raw = keep.tile([P, PACK, N], F32, name="w1_raw", tag="d_word_tab", align_bytes=64)
+        nc.sync.dma_start(w1_raw[:], w1.rearrange("(p j) n -> p j n", j=PACK))
+        xq_words = keep.tile([P, S], U32, name="xq_words", align_bytes=64)
+        nc.vector.tensor_copy(xq_words[:], x_word_tab[:].indirect(offs_t[:]))
         d_dealt = keep.tile([P, H], U32, name="d_dealt", align_bytes=64)
         nc.vector.tensor_copy(
             d_dealt[:].rearrange("p (t c i) -> p c t i", t=PACK, i=4),
             d_picked[:].rearrange("p (c i t) -> p c t i", t=PACK, i=4),
         )
-        xq_plane = keep.tile([P, S], U8, name="xq_plane", align_bytes=64)
-        nc.vector.tensor_copy(xq_plane[:], x_byte_tab[:].indirect(offs_t[:]))
-        xq_words = keep.tile([P, S], U32, name="xq_words", align_bytes=64)
-        nc.vector.tensor_copy(xq_words[:], x_word_tab[:].indirect(offs_t[:]))
+        d_plane = keep.tile([P, H], U8, name="d_plane", align_bytes=64)
+        nc.vector.tensor_copy(
+            d_plane[:].rearrange("p (t m) -> p t m", t=PACK),
+            planes[:, 0:S].rearrange("p (m t) -> p t m", t=PACK),
+        )
 
-        s_bank = [psum.tile([P, S], F32, name="s_bank%d" % t) for t in range(PACK)]
+        s_bank = [psum.tile([P, S], F32, name="s_bank%d" % t, tag="bank%d" % t) for t in range(PACK)]
         for t in range(PACK):
             cols = slice(P * t, P * (t + 1))
             nc.tensor.matmul_mx(
@@ -106,15 +111,13 @@ def tile_picked_kmixcubegmaxd_none_p_kernel(
                 lhsT=d_dealt[:, cols].bitcast(FP8X4),
                 lhsT_scale=d_plane[:, cols],
                 rhs=xq_words[:].bitcast(FP8X4),
-                rhs_scale=xq_plane[:],
+                rhs_scale=xq_plane,
                 start=True,
                 stop=True,
             )
 
         x2_words = keep.tile([P, S], U32, name="x2_words", align_bytes=64)
         nc.vector.tensor_copy(x2_words[:], x_word_tab[:].indirect(two_t[:]))
-        x2_plane = keep.tile([P, S], U8, name="x2_plane", align_bytes=64)
-        nc.vector.tensor_copy(x2_plane[:], x_byte_tab[:].indirect(two_t[:]))
 
         def interleaved(dst, src):
             return (
@@ -126,84 +129,112 @@ def tile_picked_kmixcubegmaxd_none_p_kernel(
             nc.vector.quantize_mx(codes.bitcast(FP8X4), plane, grouped.rearrange("p n t -> p (n t)"))
 
         w2_grouped = keep.tile([P, N, PACK], BF16, name="w2_grouped", align_bytes=64)
-        nc.vector.tensor_copy(*interleaved(w2_grouped[:], w2_raw))
-
+        w1_grouped = keep.tile([P, N, PACK], BF16, name="w1_grouped", align_bytes=64)
+        NP = len(PIECES)
+        width = [b - a for a, b in PIECES]
         s_row = [keep.tile([P, S], F32, name="s_row%d" % t) for t in range(PACK)]
         tanh_row = [keep.tile([P, S], F32, name="tanh_row%d" % t) for t in range(PACK)]
-        s_at_n1 = [[keep.tile([P, HALF], F32, name="s_at_n1_%d%d" % (t, u)) for u in range(2)] for t in range(PACK)]
-        pair = [[keep.tile([P, HALF], F32, name="pair_%d%d" % (t, u)) for u in range(2)] for t in range(PACK)]
-        z_half = [keep.tile([P, PACK, HALF], F32, name="z_half%d" % u) for u in range(2)]
-        z_grouped = [keep.tile([P, HALF, PACK], BF16, name="z_grouped%d" % u, align_bytes=64) for u in range(2)]
-        z_words = [keep.tile([P, HALF], U32, name="z_words%d" % u, align_bytes=64) for u in range(2)]
-        z_plane = [keep.tile([P, HALF], U8, name="z_plane%d" % u, align_bytes=64) for u in range(2)]
-        w_words = [keep.tile([P, N], U32, name="w_words%d" % i, align_bytes=64) for i in range(2)]
-        w_plane = [keep.tile([P, N], U8, name="w_plane%d" % i, align_bytes=64) for i in range(2)]
+        s_at_n1 = [[keep.tile([P, width[u]], F32, name="s_at_n1_%d%d" % (t, u)) for u in range(NP)] for t in range(PACK)]
+        pair = [[keep.tile([P, width[u]], F32, name="pair_%d%d" % (t, u)) for u in range(NP)] for t in range(PACK)]
+        z_piece = [keep.tile([P, PACK, width[u]], F32, name="z_piece%d" % u) for u in range(NP)]
+        z_grouped = [keep.tile([P, width[u], PACK], BF16, name="z_grouped%d" % u, align_bytes=64) for u in range(NP)]
+        z_words = [keep.tile([P, width[u]], U32, name="z_words%d" % u, align_bytes=64) for u in range(NP)]
+        z_plane = [keep.tile([P, width[u]], U8, name="z_plane%d" % u, align_bytes=64) for u in range(NP)]
+        w1_words = keep.tile([P, N], U32, name="w1_words", align_bytes=64)
+        w2_words = keep.tile([P, N], U32, name="w2_words", align_bytes=64)
+        w1_plane = keep.tile([P, N], U8, name="w1_plane", align_bytes=64)
+        w2_plane = keep.tile([P, N], U8, name="w2_plane", align_bytes=64)
+        h_row = [keep.tile([P, H_WINDOW], F32, name="h_row%d" % t) for t in range(N // P)]
+        for mt in range(N // P):
+            nc.gpsimd.memset(h_row[mt][:, S:], 0.0)
 
-        def fetch(t, u):
-            nc.scalar.activation(s_at_n1[t][u][:], s_row[t][:].indirect(entries(n1_t, u * HALF, HALF)), ACT.Copy)
-            nc.vector.tensor_tensor(
-                pair[t][u][:], tanh_row[t][:].indirect(entries(n2_t, u * HALF, HALF)), s_at_n1[t][u][:], ALU.mult
-            )
+        def fetch(t, u, fused):
+            a = PIECES[u][0]
+            nc.scalar.activation(s_at_n1[t][u][:], s_row[t][:].indirect(entries(n1_t, a, width[u])), ACT.Copy)
+            tanh_at_n2 = tanh_row[t][:].indirect(entries(n2_t, a, width[u]))
+            if not fused:
+                fetched = keep.tile([P, width[u]], F32, name="tanh_at_n2_%d%d" % (t, u))
+                nc.scalar.activation(fetched[:], tanh_at_n2, ACT.Copy)
+                tanh_at_n2 = fetched[:]
+            nc.vector.tensor_tensor(pair[t][u][:], tanh_at_n2, s_at_n1[t][u][:], ALU.mult)
 
         def finish(t, u):
+            a, b = PIECES[u]
             nc.vector.scalar_tensor_tensor(
-                z_half[u][:, t, :],
-                s_row[t][:, u * HALF : (u + 1) * HALF],
-                gain[:, t : t + 1],
-                pair[t][u][:],
-                ALU.mult,
-                ALU.mult,
+                z_piece[u][:, t, :], s_row[t][:, a:b], gain[:, t : t + 1], pair[t][u][:], ALU.mult, ALU.mult
             )
 
-        h_bank = [psum.tile([P, S], F32, name="h_bank%d" % t) for t in range(N // P)]
-
-        for t in range(PACK):
-            nc.scalar.activation(tanh_row[t][:], s_bank[t][:], ACT.Tanh, scale=0.0625)
-            nc.scalar.activation(s_row[t][:], s_bank[t][:], ACT.Copy, scale=0.0625)
-            fetch(t, 0)
-            if t == 0:
-                quantise(w_words[1][:], w_plane[1][:], w2_grouped[:])
-            else:
-                finish(t - 1, 0)
-        for mt in range(N // P):
+        def mx_pass(bank, mt, w_words, w_plane, words, plane, first):
             cols = slice(P * mt, P * (mt + 1))
             nc.tensor.matmul_mx(
-                h_bank[mt][:],
-                lhsT=w_words[1][:, cols].bitcast(FP8X4),
-                lhsT_scale=w_plane[1][:, cols],
-                rhs=x2_words[:].bitcast(FP8X4),
-                rhs_scale=x2_plane[:],
-                start=True,
-                stop=False,
+                bank,
+                lhsT=w_words[:, cols].bitcast(FP8X4),
+                lhsT_scale=w_plane[:, cols],
+                rhs=words.bitcast(FP8X4),
+                rhs_scale=plane,
+                start=first,
+                stop=not first,
             )
+
+        h_bank = {}
+
+        def open_h(u, tag0):
+            a, b = PIECES[u]
+            for mt in range(N // P):
+                h_bank[u, mt] = psum.tile([P, width[u]], F32, name="h_bank%d%d" % (u, mt), tag="bank%d" % (tag0 + mt))
+                mx_pass(h_bank[u, mt][:], mt, w2_words, w2_plane, x2_words[:, a:b], x2_plane[:, a:b], True)
+
+        def close_h(u):
+            for mt in range(N // P):
+                mx_pass(h_bank[u, mt][:], mt, w1_words, w1_plane, z_words[u][:], z_plane[u][:], False)
+
+        def evac(u, mt, on_vector):
+            a, b = PIECES[u]
+            if on_vector:
+                nc.vector.tensor_copy(h_row[mt][:, a:b], h_bank[u, mt][:])
+            else:
+                nc.scalar.copy(h_row[mt][:, a:b], h_bank[u, mt][:])
+
         for t in range(PACK):
-            fetch(t, 1)
             if t == 0:
-                finish(PACK - 1, 0)
+                nc.scalar.activation(tanh_row[t][:], s_bank[t][:], ACT.Tanh, scale=0.0625)
+            nc.scalar.activation(s_row[t][:], s_bank[t][:], ACT.Copy, scale=0.0625)
+            if t > 0:
+                nc.scalar.activation(tanh_row[t][:], s_bank[t][:], ACT.Tanh, scale=0.0625)
+            fetch(t, 0, True)
+            if t == 0:
+                nc.vector.tensor_copy(*interleaved(w2_grouped[:], w2_raw[:]))
+            else:
+                finish(t - 1, 0)
+            if t == 1:
+                quantise(w2_words[:], w2_plane[:], w2_grouped[:])
+            if t == 2:
+                nc.vector.tensor_copy(*interleaved(w1_grouped[:], w1_raw[:]))
+            if t == 3:
+                quantise(w1_words[:], w1_plane[:], w1_grouped[:])
+        finish(PACK - 1, 0)
+        open_h(0, 4)
+        open_h(1, 0)
+        for t in range(PACK):
+            fetch(t, 1, t < 2)
+            if t == 0:
+                nc.vector.tensor_copy(*interleaved(z_grouped[0][:], z_piece[0][:]))
             else:
                 finish(t - 1, 1)
-        w1_grouped = keep.tile([P, N, PACK], BF16, name="w1_grouped", align_bytes=64)
-        nc.scalar.copy(*interleaved(w1_grouped[:], w1_raw))
-        nc.scalar.copy(*interleaved(z_grouped[0][:], z_half[0][:]))
-        quantise(w_words[0][:], w_plane[0][:], w1_grouped[:])
+            if t == 1:
+                quantise(z_words[0][:], z_plane[0][:], z_grouped[0][:])
+                close_h(0)
         finish(PACK - 1, 1)
-        quantise(z_words[0][:], z_plane[0][:], z_grouped[0][:])
-        nc.vector.tensor_copy(*interleaved(z_grouped[1][:], z_half[1][:]))
+        for mt in range(N // P):
+            evac(0, mt, False)
+        nc.vector.tensor_copy(*interleaved(z_grouped[1][:, :160, :], z_piece[1][:, :, :160]))
+        nc.scalar.copy(*interleaved(z_grouped[1][:, 160:, :], z_piece[1][:, :, 160:]))
         quantise(z_words[1][:], z_plane[1][:], z_grouped[1][:])
-        for u in range(2):
-            for mt in range(N // P):
-                cols = slice(P * mt, P * (mt + 1))
-                nc.tensor.matmul_mx(
-                    h_bank[mt][:, u * HALF : (u + 1) * HALF],
-                    lhsT=w_words[0][:, cols].bitcast(FP8X4),
-                    lhsT_scale=w_plane[0][:, cols],
-                    rhs=z_words[u][:].bitcast(FP8X4),
-                    rhs_scale=z_plane[u][:],
-                    start=False,
-                    stop=(u == 1),
-                )
+        close_h(1)
+        evac(1, 0, True)
+        evac(1, 1, False)
+        evac(1, 3, True)
 
-        h_row = [keep.tile([P, S], F32, name="h_row%d" % t) for t in range(N // P)]
         members = [keep.tile([P, G], F32, name="members%d" % t) for t in range(N // P)]
         max2 = [keep.tile([P, G // 2], F32, name="max2_%d" % t) for t in range(N // P)]
         max4 = [keep.tile([P, S], F32, name="max4_%d" % t) for t in range(N // P)]
@@ -233,16 +264,13 @@ def tile_picked_kmixcubegmaxd_none_p_kernel(
 
         def gather_span(on_vector, mt, first, end):
             while first < end:
-                count = min(416, end - first)
+                count = min(1024, end - first)
                 gather(on_vector, mt, first, count)
                 first = first + count
 
-        nc.vector.tensor_copy(h_row[0][:], h_bank[0][:])
-        nc.scalar.copy(h_row[1][:], h_bank[1][:])
-        nc.vector.tensor_copy(h_row[3][:], h_bank[3][:])
         gather_span(False, 1, 0, G)
         gather_span(True, 0, 0, G)
-        nc.scalar.copy(h_row[2][:], h_bank[2][:])
+        evac(NP - 1, 2, False)
         gather_span(False, 2, 0, G)
         step1(0, 0, S)
         step1(1, 0, S)
@@ -250,17 +278,19 @@ def tile_picked_kmixcubegmaxd_none_p_kernel(
         step2(1, 0, S)
         step3(0, 0, S)
         step3(1, 0, S)
-        gather_span(True, 3, 0, 384)
-        gather_span(False, 3, 384, G)
+        gather_span(True, 3, 0, 320)
+        gather_span(False, 3, 320, 1024)
+        gather_span(False, 3, 1024, 1728)
+        gather_span(False, 3, 1728, G)
         step1(2, 0, S)
-        step1(3, 0, 192)
+        step1(3, 0, 256)
         step2(2, 0, S)
-        step2(3, 0, 192)
+        step2(3, 0, 256)
         step3(2, 0, S)
-        step1(3, 192, 384)
-        step3(3, 0, 192)
-        step2(3, 192, 384)
-        step1(3, 384, S)
-        step3(3, 192, 384)
-        step2(3, 384, S)
-        step3(3, 384, S)
+        step1(3, 256, 432)
+        step3(3, 0, 256)
+        step2(3, 256, 432)
+        step1(3, 432, S)
+        step3(3, 256, 432)
+        step2(3, 432, S)
+        step3(3, 432, S)

@@ -81,9 +81,9 @@ def tile_picked_kmixcubegmaxd_none_p_kernel(
 
         move_rows(nc.scalar, planes, picked_bytes)
         nc.vector.tensor_copy(x2_bytes[:], x_byte_tab[:].indirect(two_t[:]))
-        move_rows(nc.sync, x2_plane, x2_bytes)
         w2_raw = keep.tile([P, PACK, N], F32, name="w2_raw", tag="x_byte_tab", align_bytes=64)
         nc.sync.dma_start(w2_raw[:], w2.rearrange("(p j) n -> p j n", j=PACK))
+        move_rows(nc.sync, x2_plane, x2_bytes)
         xq_plane = planes[:, S : 2 * S]
 
         d_picked = keep.tile([P, H], U32, name="d_picked", align_bytes=64)
@@ -125,6 +125,17 @@ def tile_picked_kmixcubegmaxd_none_p_kernel(
                 src.rearrange("p t (c i) -> p c t i", i=4),
             )
 
+        def round_weights(grouped, raw):
+            for c0 in range(0, N, 128):
+                nc.gpsimd.tensor_scalar(
+                    grouped[:, c0 : c0 + 128, :],
+                    raw[:, :, c0 : c0 + 128].rearrange("p t n -> p n t"),
+                    1.0,
+                    0.0,
+                    ALU.mult,
+                    ALU.add,
+                )
+
         def quantise(codes, plane, grouped):
             nc.vector.quantize_mx(codes.bitcast(FP8X4), plane, grouped.rearrange("p n t -> p (n t)"))
 
@@ -161,7 +172,7 @@ def tile_picked_kmixcubegmaxd_none_p_kernel(
         def finish(t, u):
             a, b = PIECES[u]
             nc.vector.scalar_tensor_tensor(
-                z_piece[u][:, t, :], s_row[t][:, a:b], gain[:, t : t + 1], pair[t][u][:], ALU.mult, ALU.mult
+                z_piece[u][:, t, :], s_bank[t][:, a:b], gain[:, t : t + 1], pair[t][u][:], ALU.mult, ALU.mult
             )
 
         def mx_pass(bank, mt, w_words, w_plane, words, plane, first):
@@ -195,40 +206,36 @@ def tile_picked_kmixcubegmaxd_none_p_kernel(
             else:
                 nc.scalar.copy(h_row[mt][:, a:b], h_bank[u, mt][:])
 
+        round_weights(w2_grouped, w2_raw)
+        round_weights(w1_grouped, w1_raw)
         for t in range(PACK):
             if t == 0:
                 nc.scalar.activation(tanh_row[t][:], s_bank[t][:], ACT.Tanh, scale=0.0625)
-            nc.scalar.activation(s_row[t][:], s_bank[t][:], ACT.Copy, scale=0.0625)
+            nc.scalar.activation(s_row[t][:], s_bank[t][:], ACT.Copy, scale=0.0625 * 0.0625)
             if t > 0:
                 nc.scalar.activation(tanh_row[t][:], s_bank[t][:], ACT.Tanh, scale=0.0625)
             fetch(t, 0, True)
-            if t == 0:
-                nc.vector.tensor_copy(*interleaved(w2_grouped[:], w2_raw[:]))
-            else:
+            if t > 0:
                 finish(t - 1, 0)
-            if t == 1:
-                quantise(w2_words[:], w2_plane[:], w2_grouped[:])
             if t == 2:
-                nc.vector.tensor_copy(*interleaved(w1_grouped[:], w1_raw[:]))
-            if t == 3:
-                quantise(w1_words[:], w1_plane[:], w1_grouped[:])
-        finish(PACK - 1, 0)
+                quantise(w2_words[:], w2_plane[:], w2_grouped[:])
         open_h(0, 4)
-        open_h(1, 0)
         for t in range(PACK):
             fetch(t, 1, t < 2)
             if t == 0:
-                nc.vector.tensor_copy(*interleaved(z_grouped[0][:], z_piece[0][:]))
+                finish(PACK - 1, 0)
+                quantise(w1_words[:], w1_plane[:], w1_grouped[:])
             else:
                 finish(t - 1, 1)
-            if t == 1:
-                quantise(z_words[0][:], z_plane[0][:], z_grouped[0][:])
-                close_h(0)
+        nc.scalar.copy(*interleaved(z_grouped[0][:], z_piece[0][:]))
         finish(PACK - 1, 1)
-        for mt in range(N // P):
-            evac(0, mt, False)
+        open_h(1, 0)
+        quantise(z_words[0][:], z_plane[0][:], z_grouped[0][:])
+        close_h(0)
         nc.vector.tensor_copy(*interleaved(z_grouped[1][:, :160, :], z_piece[1][:, :, :160]))
         nc.scalar.copy(*interleaved(z_grouped[1][:, 160:, :], z_piece[1][:, :, 160:]))
+        for mt in range(N // P):
+            evac(0, mt, False)
         quantise(z_words[1][:], z_plane[1][:], z_grouped[1][:])
         close_h(1)
         evac(1, 0, True)

from contextlib import ExitStack

import concourse.mybir as mybir

K, T, S, N, G, H = 512, 2048, 512, 512, 2048, 512
FLOPS = 3 * 2 * 512 * 512 * 512

F32 = mybir.dt.float32
BF16 = mybir.dt.bfloat16
U32 = mybir.dt.uint32
I32 = mybir.dt.int32
U16 = mybir.dt.uint16
U8 = mybir.dt.uint8
FP8X4 = mybir.dt.float8_e4m3fn_x4
ALU = mybir.AluOpType
ACT = mybir.ActivationFunctionType

P = 128
PACK = 4
PIECES = ((0, 256), (256, 512))
MEMBERS = 4
H_WINDOW = 1056


def entries(list_tile, first, count):
    return list_tile[:, first // 16 : (first + count) // 16]


def tile_picked_kmixcubegmaxd_none_p_kernel(
    tc, x_words, x_scales, d_words, d_scales, gn, w1, w2, offs, k1, n1, n2, two, n3, out
):
    nc = tc.nc
    with ExitStack() as ctx:
        keep = ctx.enter_context(tc.tile_pool(name="keep", bufs=1))
        psum = ctx.enter_context(tc.psum_pool(name="psum", bufs=1))

        def list_tile(name, src):
            tile = keep.tile(list(src.shape), U16, name=name)
            nc.sync.dma_start(tile[:], src)
            return tile

        def word_table(name, src):
            tile = keep.tile([P, T], U32, name=name, tag=name, align_bytes=64)
            nc.sync.dma_start(tile[:].bitcast(I32), src[0].rearrange("p n t -> p (n t)").bitcast(I32))
            return tile

        def byte_table(name, src):
            tile = keep.tile([P, T], U8, name=name, tag=name, align_bytes=64)
            nc.sync.dma_start(tile[:].bitcast(I32), src[0].bitcast(I32).unsqueeze(1).to_broadcast([16, 8, T // 4]))
            return tile

        planes = keep.tile([P, 2 * S], U8, name="planes", align_bytes=64)
        nc.vector.memset(planes[:].bitcast(I32), 0)
        x2_plane = keep.tile([P, S], U8, name="x2_plane", align_bytes=64)
        nc.vector.memset(x2_plane[:].bitcast(I32), 0)

        k1_t = list_tile("k1_t", k1)
        d_byte_tab = byte_table("d_byte_tab", d_scales)
        offs_t = list_tile("offs_t", offs)
        x_byte_tab = byte_table("x_byte_tab", x_scales)
        two_t = list_tile("two_t", two)
        d_word_tab = word_table("d_word_tab", d_words)
        n1_t = list_tile("n1_t", n1)
        n2_t = list_tile("n2_t", n2)
        x_word_tab = word_table("x_word_tab", x_words)
        n3_t = list_tile("n3_t", n3)
        gain = keep.tile([P, PACK], F32, name="gain")
        nc.sync.dma_start(gain[:], gn.rearrange("(p t) o -> p (t o)", t=PACK))

        picked_bytes = keep.tile([P, 2 * S], U8, name="picked_bytes", align_bytes=64)
        x2_bytes = keep.tile([P, S], U8, name="x2_bytes", align_bytes=64)
        nc.vector.tensor_copy(picked_bytes[:, 0:S], d_byte_tab[:].indirect(k1_t[:]))
        nc.vector.tensor_copy(picked_bytes[:, S : 2 * S], x_byte_tab[:].indirect(offs_t[:]))

        def move_rows(queue, dst, src):
            for a in range(4):
                queue.dma_start(
                    dst[:].bitcast(I32)[a:P:32, :],
                    src[:].bitcast(I32)[8 * a : P : 32, :],
                )

        move_rows(nc.scalar, planes, picked_bytes)
        nc.vector.tensor_copy(x2_bytes[:], x_byte_tab[:].indirect(two_t[:]))
        w2_raw = keep.tile([P, PACK, N], F32, name="w2_raw", tag="x_byte_tab", align_bytes=64)
        nc.sync.dma_start(w2_raw[:], w2.rearrange("(p j) n -> p j n", j=PACK))
        move_rows(nc.sync, x2_plane, x2_bytes)
        xq_plane = planes[:, S : 2 * S]

        d_picked = keep.tile([P, H], U32, name="d_picked", align_bytes=64)
        nc.vector.tensor_copy(d_picked[:], d_word_tab[:].indirect(k1_t[:]))
        w1_raw = keep.tile([P, PACK, N], F32, name="w1_raw", tag="d_word_tab", align_bytes=64)
        nc.sync.dma_start(w1_raw[:], w1.rearrange("(p j) n -> p j n", j=PACK))
        xq_words = keep.tile([P, S], U32, name="xq_words", align_bytes=64)
        nc.vector.tensor_copy(xq_words[:], x_word_tab[:].indirect(offs_t[:]))
        d_dealt = keep.tile([P, H], U32, name="d_dealt", align_bytes=64)
        nc.vector.tensor_copy(
            d_dealt[:].rearrange("p (t c i) -> p c t i", t=PACK, i=4),
            d_picked[:].rearrange("p (c i t) -> p c t i", t=PACK, i=4),
        )
        d_plane = keep.tile([P, H], U8, name="d_plane", align_bytes=64)
        nc.vector.tensor_copy(
            d_plane[:].rearrange("p (t m) -> p t m", t=PACK),
            planes[:, 0:S].rearrange("p (m t) -> p t m", t=PACK),
        )

        s_bank = [psum.tile([P, S], F32, name="s_bank%d" % t, tag="bank%d" % t) for t in range(PACK)]
        for t in range(PACK):
            cols = slice(P * t, P * (t + 1))
            nc.tensor.matmul_mx(
                s_bank[t][:],
                lhsT=d_dealt[:, cols].bitcast(FP8X4),
                lhsT_scale=d_plane[:, cols],
                rhs=xq_words[:].bitcast(FP8X4),
                rhs_scale=xq_plane,
                start=True,
                stop=True,
            )

        x2_words = keep.tile([P, S], U32, name="x2_words", align_bytes=64)
        nc.vector.tensor_copy(x2_words[:], x_word_tab[:].indirect(two_t[:]))

        def interleaved(dst, src):
            return (
                dst.rearrange("p (c i) t -> p c t i", i=4),
                src.rearrange("p t (c i) -> p c t i", i=4),
            )

        def round_weights(grouped, raw):
            for c0 in range(0, N, 128):
                nc.gpsimd.tensor_scalar(
                    grouped[:, c0 : c0 + 128, :],
                    raw[:, :, c0 : c0 + 128].rearrange("p t n -> p n t"),
                    1.0,
                    0.0,
                    ALU.mult,
                    ALU.add,
                )

        def quantise(codes, plane, grouped):
            nc.vector.quantize_mx(codes.bitcast(FP8X4), plane, grouped.rearrange("p n t -> p (n t)"))

        w2_grouped = keep.tile([P, N, PACK], BF16, name="w2_grouped", align_bytes=64)
        w1_grouped = keep.tile([P, N, PACK], BF16, name="w1_grouped", align_bytes=64)
        NP = len(PIECES)
        width = [b - a for a, b in PIECES]
        s_row = [keep.tile([P, S], F32, name="s_row%d" % t) for t in range(PACK)]
        tanh_row = [keep.tile([P, S], F32, name="tanh_row%d" % t) for t in range(PACK)]
        s_at_n1 = [[keep.tile([P, width[u]], F32, name="s_at_n1_%d%d" % (t, u)) for u in range(NP)] for t in range(PACK)]
        pair = [[keep.tile([P, width[u]], F32, name="pair_%d%d" % (t, u)) for u in range(NP)] for t in range(PACK)]
        z_piece = [keep.tile([P, PACK, width[u]], F32, name="z_piece%d" % u) for u in range(NP)]
        z_grouped = [keep.tile([P, width[u], PACK], BF16, name="z_grouped%d" % u, align_bytes=64) for u in range(NP)]
        z_words = [keep.tile([P, width[u]], U32, name="z_words%d" % u, align_bytes=64) for u in range(NP)]
        z_plane = [keep.tile([P, width[u]], U8, name="z_plane%d" % u, align_bytes=64) for u in range(NP)]
        w1_words = keep.tile([P, N], U32, name="w1_words", align_bytes=64)
        w2_words = keep.tile([P, N], U32, name="w2_words", align_bytes=64)
        w1_plane = keep.tile([P, N], U8, name="w1_plane", align_bytes=64)
        w2_plane = keep.tile([P, N], U8, name="w2_plane", align_bytes=64)
        h_row = [keep.tile([P, H_WINDOW], F32, name="h_row%d" % t) for t in range(N // P)]
        for mt in range(N // P):
            nc.gpsimd.memset(h_row[mt][:, S:], 0.0)

        def fetch(t, u, fused):
            a = PIECES[u][0]
            nc.scalar.activation(s_at_n1[t][u][:], s_row[t][:].indirect(entries(n1_t, a, width[u])), ACT.Copy)
            tanh_at_n2 = tanh_row[t][:].indirect(entries(n2_t, a, width[u]))
            if not fused:
                fetched = keep.tile([P, width[u]], F32, name="tanh_at_n2_%d%d" % (t, u))
                nc.scalar.activation(fetched[:], tanh_at_n2, ACT.Copy)
                tanh_at_n2 = fetched[:]
            nc.vector.tensor_tensor(pair[t][u][:], tanh_at_n2, s_at_n1[t][u][:], ALU.mult)

        def finish(t, u):
            a, b = PIECES[u]
            nc.vector.scalar_tensor_tensor(
                z_piece[u][:, t, :], s_bank[t][:, a:b], gain[:, t : t + 1], pair[t][u][:], ALU.mult, ALU.mult
            )

        def mx_pass(bank, mt, w_words, w_plane, words, plane, first):
            cols = slice(P * mt, P * (mt + 1))
            nc.tensor.matmul_mx(
                bank,
                lhsT=w_words[:, cols].bitcast(FP8X4),
                lhsT_scale=w_plane[:, cols],
                rhs=words.bitcast(FP8X4),
                rhs_scale=plane,
                start=first,
                stop=not first,
            )

        h_bank = {}

        def open_h(u, tag0):
            a, b = PIECES[u]
            for mt in range(N // P):
                h_bank[u, mt] = psum.tile([P, width[u]], F32, name="h_bank%d%d" % (u, mt), tag="bank%d" % (tag0 + mt))
                mx_pass(h_bank[u, mt][:], mt, w2_words, w2_plane, x2_words[:, a:b], x2_plane[:, a:b], True)

        def close_h(u):
            for mt in range(N // P):
                mx_pass(h_bank[u, mt][:], mt, w1_words, w1_plane, z_words[u][:], z_plane[u][:], False)

        def evac(u, mt, on_vector):
            a, b = PIECES[u]
            if on_vector:
                nc.vector.tensor_copy(h_row[mt][:, a:b], h_bank[u, mt][:])
            else:
                nc.scalar.copy(h_row[mt][:, a:b], h_bank[u, mt][:])

        round_weights(w2_grouped, w2_raw)
        round_weights(w1_grouped, w1_raw)
        for t in range(PACK):
            if t == 0:
                nc.scalar.activation(tanh_row[t][:], s_bank[t][:], ACT.Tanh, scale=0.0625)
            nc.scalar.activation(s_row[t][:], s_bank[t][:], ACT.Copy, scale=0.0625 * 0.0625)
            if t > 0:
                nc.scalar.activation(tanh_row[t][:], s_bank[t][:], ACT.Tanh, scale=0.0625)
            fetch(t, 0, True)
            if t > 0:
                finish(t - 1, 0)
            if t == 2:
                quantise(w2_words[:], w2_plane[:], w2_grouped[:])
        open_h(0, 4)
        for t in range(PACK):
            fetch(t, 1, t < 2)
            if t == 0:
                finish(PACK - 1, 0)
                quantise(w1_words[:], w1_plane[:], w1_grouped[:])
            else:
                finish(t - 1, 1)
        nc.scalar.copy(*interleaved(z_grouped[0][:], z_piece[0][:]))
        finish(PACK - 1, 1)
        open_h(1, 0)
        quantise(z_words[0][:], z_plane[0][:], z_grouped[0][:])
        close_h(0)
        nc.vector.tensor_copy(*interleaved(z_grouped[1][:, :160, :], z_piece[1][:, :, :160]))
        nc.scalar.copy(*interleaved(z_grouped[1][:, 160:, :], z_piece[1][:, :, 160:]))
        for mt in range(N // P):
            evac(0, mt, False)
        quantise(z_words[1][:], z_plane[1][:], z_grouped[1][:])
        close_h(1)
        evac(1, 0, True)
        evac(1, 1, False)
        evac(1, 3, True)

        members = [keep.tile([P, G], F32, name="members%d" % t) for t in range(N // P)]
        max2 = [keep.tile([P, G // 2], F32, name="max2_%d" % t) for t in range(N // P)]
        max4 = [keep.tile([P, S], F32, name="max4_%d" % t) for t in range(N // P)]
        result = [keep.tile([P, S], F32, name="result%d" % t) for t in range(N // P)]

        def gather(on_vector, mt, first, count):
            src = h_row[mt][:].indirect(entries(n3_t, first, count))
            dst = members[mt][:, first : first + count]
            if on_vector:
                nc.vector.tensor_copy(dst, src)
            else:
                nc.scalar.activation(dst, src, ACT.Copy)

        def step1(mt, j0, j1):
            g = members[mt][:, 4 * j0 : 4 * j1].rearrange("p (j a b) -> p j a b", a=2, b=2)
            nc.vector.tensor_tensor(
                max2[mt][:, 2 * j0 : 2 * j1].rearrange("p (j b) -> p j b", b=2), g[:, :, 0, :], g[:, :, 1, :], ALU.max
            )

        def step2(mt, j0, j1):
            g = max2[mt][:, 2 * j0 : 2 * j1].rearrange("p (j b) -> p j b", b=2)
            nc.vector.tensor_tensor(max4[mt][:, j0:j1], g[:, :, 0], g[:, :, 1], ALU.max)

        def step3(mt, j0, j1):
            nc.vector.tensor_tensor(result[mt][:, j0:j1], h_row[mt][:, j0:j1], max4[mt][:, j0:j1], ALU.subtract)
            nc.sync.dma_start(out[P * mt : P * (mt + 1), j0:j1], result[mt][:, j0:j1])

        def gather_span(on_vector, mt, first, end):
            while first < end:
                count = min(1024, end - first)
                gather(on_vector, mt, first, count)
                first = first + count

        gather_span(False, 1, 0, G)
        gather_span(True, 0, 0, G)
        evac(NP - 1, 2, False)
        gather_span(False, 2, 0, G)
        step1(0, 0, S)
        step1(1, 0, S)
        step2(0, 0, S)
        step2(1, 0, S)
        step3(0, 0, S)
        step3(1, 0, S)
        gather_span(True, 3, 0, 320)
        gather_span(False, 3, 320, 1024)
        gather_span(False, 3, 1024, 1728)
        gather_span(False, 3, 1728, G)
        step1(2, 0, S)
        step1(3, 0, 256)
        step2(2, 0, S)
        step2(3, 0, 256)
        step3(2, 0, S)
        step1(3, 256, 432)
        step3(3, 0, 256)
        step2(3, 256, 432)
        step1(3, 432, S)
        step3(3, 256, 432)
        step2(3, 432, S)
        step3(3, 432, S)
